import numpy as np
import ml_dtypes


def mxq(x, axis, fmt="e4m3"):
    dtype, down = {"e4m3": (ml_dtypes.float8_e4m3fn, 7), "e5m2": (ml_dtypes.float8_e5m2, 14)}[fmt]
    v = np.moveaxis(np.asarray(x, np.float32).astype(ml_dtypes.bfloat16).astype(np.float64), axis, -1)
    blocks = v.reshape(v.shape[:-1] + (-1, 32))
    amax = np.abs(blocks).max(-1, keepdims=True)
    byte = np.maximum(np.where(amax > 0, np.frexp(amax)[1] - 1 + 127, 0) - down, 1)
    scale = np.exp2(byte - 127.0)
    codes = (blocks / scale).astype(np.float32).astype(dtype).astype(np.float64)
    return np.moveaxis((codes * scale).reshape(v.shape), -1, axis)


WIDE = False


def mx_kscale(k):
    if not WIDE:
        return np.ones(k)
    levels = np.array([10, -10, 5, -5, 0])
    if k % 512:
        return np.exp2(np.random.permutation(np.resize(levels, k // 32))).repeat(32)
    a = np.empty((k // 512, 16))
    for p in range(k // 512):
        a[p, :8] = np.random.permutation(np.resize(levels, 8))
        for g in range(8):
            far = levels[np.abs(levels - a[p, g]) >= 10]
            a[p, g + 8] = far[np.random.randint(len(far))]
    return np.exp2(a.ravel()).repeat(32)


BF16 = ml_dtypes.bfloat16


def bf(x):
    return np.asarray(x, np.float32).astype(BF16)


def f64(x):
    return np.asarray(x).astype(np.float64)


E2M1 = np.array([0.0, 0.5, 1.0, 1.5, 2.0, 3.0, 4.0, 6.0, -0.0, -0.5, -1.0, -1.5, -2.0, -3.0, -4.0, -6.0])


def pack_weight(w, fmt):
    k, n = w.shape
    w = f64(bf(w)).reshape(k // 32, 32, n)
    amax = np.abs(w).max(1)
    if fmt == "e4m3":
        byte = np.frexp(amax)[1] - 1 + 127 - 7
    else:
        mant, ex = np.frexp(amax / 6.0)
        byte = np.where(mant > 0.5, ex, ex - 1) + 127
    byte = np.clip(np.where(amax > 0, byte, 1), 1, 254)
    scaled = (w * np.exp2(127.0 - byte)[:, None, :]).reshape(k, n).astype(np.float32)
    by_word = np.ascontiguousarray(scaled.reshape(k // 512, 128, 4, n).transpose(0, 1, 3, 2))
    if fmt == "e4m3":
        words = by_word.astype(ml_dtypes.float8_e4m3fn).view(np.uint8)
    else:
        c = by_word.astype(ml_dtypes.float4_e2m1fn).view(np.uint8) & 0xF
        words = c[..., 0::2] | (c[..., 1::2] << 4)
    return np.ascontiguousarray(words), np.ascontiguousarray(byte.astype(np.uint8).reshape(k // 512, 16, n))


def unpack_weight(words, scales, fmt):
    g, p, n, _ = words.shape
    if fmt == "e4m3":
        vals = np.ascontiguousarray(words).view(ml_dtypes.float8_e4m3fn).astype(np.float64)
    else:
        nib = np.empty((g, p, n, 4), np.uint8)
        nib[..., 0::2] = words & 0xF
        nib[..., 1::2] = words >> 4
        vals = E2M1[nib]
    vals = vals * np.repeat(np.exp2(scales.astype(np.float64) - 127.0), 8, axis=1)[..., None]
    return vals.transpose(0, 1, 3, 2).reshape(g * 512, n)
def pack4(w):
    words, scales = pack_weight(w, "e2m1")
    return words.reshape(words.shape[0], 128, -1), scales


def unpack4(words, scales):
    return unpack_weight(words.reshape(words.shape[0], 128, -1, 2), scales, "e2m1")


def planes(Y):
    n, m = Y.shape
    b = f64(bf(Y)).reshape(n // 32, 32, m)
    amax = np.abs(b).max(1)
    byte = np.clip(np.where(amax > 0, np.frexp(amax)[1] - 1 + 127 - 7, 1), 1, 254)
    codes = (b * np.exp2(127.0 - byte)[:, None, :]).reshape(n, m).astype(np.float32).astype(ml_dtypes.float8_e4m3fn).view(np.uint8)
    words = codes.reshape(n // 512, 128, 4, m).transpose(0, 1, 3, 2)
    return np.ascontiguousarray(words), np.ascontiguousarray(byte.astype(np.uint8).reshape(n // 512, 16, m))


T, K, P, C = 1024, 2048, 1024, 1536

def setup_inputs():
    s = mx_kscale(K)
    t = mx_kscale(P)
    limit = np.exp(0.7 * np.random.randn(C))
    magnetics = np.random.randn(T, K) * s[None, :]
    response = np.random.randn(K, P) / np.sqrt(K) / s[:, None]
    target = np.random.randn(T, P)
    signal_weight = np.exp(0.3 * np.random.randn(P)) * t
    gain = 0.7 * np.random.randn(P, C) / np.sqrt(P) * limit[None, :] / t[:, None]
    feedforward = 0.3 * np.random.randn(C) * limit
    response_words, response_scales = pack4(response)
    gain_words, gain_scales = pack4(gain)
    return {
        "magnetics": bf(magnetics),
        "response_words": response_words,
        "response_scales": response_scales,
        "target": bf(target),
        "signal_weight": bf(signal_weight),
        "gain_words": gain_words,
        "gain_scales": gain_scales,
        "feedforward": bf(feedforward),
        "current_limit": bf(limit),
    }

def reference(magnetics, response_words, response_scales, target, signal_weight, gain_words, gain_scales, feedforward, current_limit):
    R = unpack4(response_words, response_scales)
    A = unpack4(gain_words, gain_scales)
    signals = mxq(f64(magnetics), 1, "e4m3") @ R
    residual = (f64(target) - signals) * f64(signal_weight)
    request = (mxq(residual, 1, "e4m3") @ A) + f64(feedforward)
    limit = f64(current_limit)
    y = limit * np.tanh(request / limit)
    words, scales = planes(y.T)
    return y, words, scales

from contextlib import ExitStack

import concourse.mybir as mybir
from concourse.masks import make_identity

T, K, P, C = 1024, 2048, 1024, 1536
FLOPS = 2 * T * K * P + 2 * T * P * C

F32 = mybir.dt.float32
BF16 = mybir.dt.bfloat16
I32 = mybir.dt.int32
U32 = mybir.dt.uint32
U8 = mybir.dt.uint8
FP8X4 = mybir.dt.float8_e4m3fn_x4
FP4X4 = mybir.dt.float4_e2m1fn_x4
ALU = mybir.AluOpType
ACT = mybir.ActivationFunctionType

PART = 128
PASS = 512
TILES = T // PART
KG, PG, CG = K // PASS, P // PASS, C // PASS
CHUNK_TILES = PASS // PART
CHUNKS = T // PASS
BANKS = 8
SORTED = (3, 4, 5, 6, 7)


def tile_magnetics_residual_coil_currents_h1_kernel(
    tc, magnetics, response_words, response_scales, target, signal_weight,
    gain_words, gain_scales, feedforward, current_limit, out_0, out_1, out_2,
):
    nc = tc.nc
    with ExitStack() as ctx:
        keep = ctx.enter_context(tc.tile_pool(name="keep", bufs=1))
        work = ctx.enter_context(tc.tile_pool(name="work", bufs=2))
        psum = ctx.enter_context(tc.psum_pool(name="psum", bufs=1))
        ctx.enter_context(tc.manual_schedule())

        held = {}
        banks_used = []

        def next_bank():
            n = len(banks_used) % BANKS
            bank = psum.tile([PART, PASS], F32, name="bank%d" % n, tag="bank%d" % n)
            banks_used.append(n)
            return bank

        def kept(name, shape, dtype):
            return keep.tile(shape, dtype, name=name, tag=name, align_bytes=256)

        def rotating(key, shape, dtype, bufs):
            held[key] = work.tile(shape, dtype, name=key[0], tag=key[0], bufs=bufs, align_bytes=256)
            return held[key]

        ident = kept("ident", [PART, PART], F32)
        r_scale = kept("r_scale", [PART, KG, P], U8)
        a_scale_raw = kept("a_scale_raw", [PART, PG, C], U8)
        warm = kept("warm", [PART, 8], F32)
        nc.vector.memset(r_scale[:].rearrange("p g n -> p (g n)").bitcast(I32), 0)
        make_identity(nc, ident[:])
        nc.vector.memset(a_scale_raw[:].rearrange("p g n -> p (g n)").bitcast(I32), 0)
        nc.scalar.activation(out=warm[:, 0:1], in_=ident[:, 0:1], func=ACT.Tanh)

        x_sb = [kept("x%d" % i, [PART, K], BF16) for i in range(TILES)]
        t_sb = [kept("t%d" % i, [PART, P], BF16) for i in range(TILES)]
        r_words = [kept("r%d" % g, [PART, 2 * P], U8) for g in range(KG)]
        a_raw = [kept("a_raw%d" % G, [PART, PG, 2 * PASS], U8) for G in range(CG)]
        w_col = kept("w_col", [PART, PG, 4], BF16)
        b_col = kept("b_col", [PART, CG, 4], BF16)
        c_col = kept("c_col", [PART, CG, 4], BF16)

        def load_x(i, pieces=1):
            width = K // pieces
            for s in range(pieces):
                cols = slice(s * width, (s + 1) * width)
                nc.sync.dma_start(out=x_sb[i][:, cols], in_=magnetics[i * PART:(i + 1) * PART, cols])

        def load_t(i):
            nc.sync.dma_start(out=t_sb[i][:], in_=target[i * PART:(i + 1) * PART, :])

        def load_scales(plane, rows):
            for q in range(4):
                nc.sync.dma_start(
                    out=plane[32 * q:32 * q + 4, :, :].bitcast(I32),
                    in_=rows[:, 4 * q:4 * q + 4, :].rearrange("g r n -> r g n").bitcast(I32),
                )

        def load_column(tile, vector):
            nc.sync.dma_start(out=tile[:], in_=vector.rearrange("(g p t) -> p g t", p=PART, t=4))

        def load_a(G):
            nc.sync.dma_start(
                out=a_raw[G][:].bitcast(I32),
                in_=gain_words[:, :, G * 2 * PASS:(G + 1) * 2 * PASS].rearrange("g p n -> p g n").bitcast(I32),
            )

        load_x(0, pieces=2)
        load_x(1)
        load_scales(r_scale, response_scales)
        for g in range(KG):
            nc.sync.dma_start(out=r_words[g][:].bitcast(I32), in_=response_words[g].bitcast(I32))
        load_column(w_col, signal_weight)
        load_x(2)
        load_t(0)
        load_scales(a_scale_raw, gain_scales)
        load_a(0)
        load_t(1)
        load_x(3)
        load_column(b_col, feedforward)
        load_column(c_col, current_limit)
        load_a(1)
        load_x(4)
        load_t(2)
        load_a(2)
        for i in range(3, TILES):
            if i + 2 < TILES:
                load_x(i + 2)
            load_t(i)

        w_row = kept("w_row", [PART, P], BF16)
        c_f32 = kept("c_f32", [PART, CG * 4], F32)
        inv_c = kept("inv_c", [PART, CG * 4], F32)
        b_over_c = kept("b_over_c", [PART, CG * 4], F32)
        a_words = kept("a_words", [PART, CG, PG, 4, PART, 2], U8)
        a_scale = kept("a_scale", [PART, CG, PG, 4, PART], U8)
        e_codes = [kept("e_codes%d" % h, [PART, PG, PASS], U32) for h in range(CHUNKS)]
        e_scale = [kept("e_scale%d" % h, [PART, PG, PASS], U8) for h in range(CHUNKS)]
        y_scale = [kept("y_scale%d" % h, [PART, CG, PASS], U8) for h in range(CHUNKS)]

        def spread_w():
            bank = next_bank()
            words = w_col[:].rearrange("p g t -> p (g t)").bitcast(F32)
            for s in range(2 * PG):
                nc.tensor.transpose(bank[:, s * PART:(s + 1) * PART], words[:, s:s + 1].to_broadcast([PART, PART]), ident[:])
            nc.scalar.copy(out=w_row[:].bitcast(F32), in_=bank[:])

        def coil_constants(stage):
            if stage == 0:
                nc.vector.tensor_copy(out=c_f32[:], in_=c_col[:].rearrange("p g t -> p (g t)"))
            elif stage == 1:
                nc.vector.reciprocal(out=inv_c[:], in_=c_f32[:])
            else:
                nc.vector.tensor_tensor(out=b_over_c[:], in0=b_col[:].rearrange("p g t -> p (g t)"), in1=inv_c[:], op=ALU.mult)

        def order_a_words(G, g):
            nc.vector.tensor_copy(
                out=a_words[:, G, g],
                in_=a_raw[G][:, g, :].rearrange("p (m t b) -> p t m b", t=4, b=2),
            )

        def order_a_scales(G):
            nc.vector.tensor_copy(
                out=a_scale[:, G],
                in_=a_scale_raw[:, :, G * PASS:(G + 1) * PASS].rearrange("p g (m t) -> p g t m", t=4),
            )

        def sort_x(i):
            ordered = rotating(("x_sorted", i), [PART, KG, 2, PART], F32, 2)
            nc.scalar.copy(out=ordered[:], in_=x_sb[i][:].bitcast(F32).rearrange("r (g p u) -> r g u p", g=KG, u=2))

        def turn_x(i, half):
            if half == 0:
                rotating(("x_grouped", i), [PART, KG, PART, 4], BF16, 2)
            bank = next_bank()
            words = x_sb[i][:].bitcast(F32)
            for s in range(4):
                g, u = 2 * half + s // 2, s % 2
                source = held[("x_sorted", i)][:, g, u, :] if i in SORTED else words[:, 256 * g + u:256 * (g + 1):2]
                nc.tensor.transpose(bank[:, s * PART:(s + 1) * PART], source, ident[:])
            grouped = held[("x_grouped", i)][:, 2 * half:2 * half + 2].rearrange("p g r t -> p (g r t)").bitcast(F32)
            nc.scalar.copy(
                out=grouped.rearrange("p (g r u) -> p g r u", g=2, u=2),
                in_=bank[:].rearrange("p (g u r) -> p g r u", g=2, u=2),
            )

        def quantise_x(i):
            codes = rotating(("x_codes", i), [PART, KG * PART], U32, 3)
            scale = rotating(("x_scale", i), [PART, KG * PART], U8, 3)
            nc.vector.quantize_mx(
                out=codes[:].bitcast(FP8X4), scales=scale[:],
                in_=held[("x_grouped", i)][:].rearrange("p g r t -> p (g r t)"),
            )

        def signals(i, g2, passes=range(KG)):
            if 0 in passes:
                held[("signals", i, g2)] = next_bank()
            bank = held[("signals", i, g2)]
            for g in passes:
                cols = slice(g * PART, (g + 1) * PART)
                nc.tensor.matmul_mx(
                    out=bank[:],
                    lhsT=held[("x_codes", i)][:, cols].bitcast(FP8X4),
                    lhsT_scale=held[("x_scale", i)][:, cols],
                    rhs=r_words[g][:, g2 * 2 * PASS:(g2 + 1) * 2 * PASS].bitcast(FP4X4),
                    rhs_scale=r_scale[:, g, g2 * PASS:(g2 + 1) * PASS],
                    start=(g == 0), stop=(g == KG - 1),
                )

        def subtract(i, g2):
            diff = rotating(("diff", i, g2), [PART, PASS], F32, 3)
            nc.vector.tensor_tensor(
                out=diff[:].rearrange("r (u p e) -> r u p e", u=2, e=2),
                in0=t_sb[i][:, g2 * PASS:(g2 + 1) * PASS].rearrange("r (p u e) -> r u p e", u=2, e=2),
                in1=held[("signals", i, g2)][:].rearrange("r (p u e) -> r u p e", u=2, e=2),
                op=ALU.subtract,
            )

        def weigh(i, g2):
            if g2 == 0:
                rotating(("resid", i), [PART, P], BF16, 3)
            cols = slice(g2 * PASS, (g2 + 1) * PASS)
            nc.vector.tensor_tensor(out=held[("resid", i)][:, cols], in0=held[("diff", i, g2)][:], in1=w_row[:, cols], op=ALU.mult)

        def turn_e(i, on_vector=False):
            bank = next_bank()
            words = held[("resid", i)][:].bitcast(F32)
            for s in range(2 * PG):
                nc.tensor.transpose(bank[:, s * PART:(s + 1) * PART], words[:, s * PART:(s + 1) * PART], ident[:])
            grouped = rotating(("e_grouped", i), [PART, PG * PASS], BF16, 2)
            (nc.vector.tensor_copy if on_vector else nc.scalar.copy)(
                out=grouped[:].bitcast(F32).rearrange("p (g r u) -> p g r u", g=PG, u=2),
                in_=bank[:].rearrange("p (g u r) -> p g r u", g=PG, u=2),
            )

        def quantise_e(i):
            h, j = divmod(i, CHUNK_TILES)
            cols = slice(j * PART, (j + 1) * PART)
            for g in range(PG):
                nc.vector.quantize_mx(
                    out=e_codes[h][:, g, cols].bitcast(FP8X4), scales=e_scale[h][:, g, cols],
                    in_=held[("e_grouped", i)][:, g * PASS:(g + 1) * PASS],
                )

        def request(h, G, t):
            bank = next_bank()
            for g in range(PG):
                nc.tensor.matmul_mx(
                    out=bank[:],
                    lhsT=a_words[:, G, g, t].rearrange("p m b -> p (m b)").bitcast(FP4X4),
                    lhsT_scale=a_scale[:, G, g, t],
                    rhs=e_codes[h][:, g, :].bitcast(FP8X4),
                    rhs_scale=e_scale[h][:, g, :],
                    start=(g == 0), stop=(g == PG - 1),
                )
            col = slice(4 * G + t, 4 * G + t + 1)
            smooth = rotating(("smooth", h, G, t), [PART, PASS], F32, 4)
            nc.scalar.activation(out=smooth[:], in_=bank[:], func=ACT.Tanh, bias=b_over_c[:, col], scale=inv_c[:, col])

        def limit(h, G, t, on_scalar=False):
            if t == 0:
                rotating(("y_t", h, G), [PART, 4, PASS], F32, 3)
            col = slice(4 * G + t, 4 * G + t + 1)
            if on_scalar:
                nc.scalar.activation(out=held[("y_t", h, G)][:, t, :], in_=held[("smooth", h, G, t)][:], func=ACT.Copy, scale=c_f32[:, col])
                return
            nc.vector.tensor_scalar(
                out=held[("y_t", h, G)][:, t, :], in0=held[("smooth", h, G, t)][:],
                scalar1=c_f32[:, col], scalar2=None, op0=ALU.mult,
            )

        def group_y(h, G):
            grouped = rotating(("y_grouped", h, G), [PART, PASS, 4], BF16, 2)
            nc.vector.tensor_copy(out=grouped[:], in_=held[("y_t", h, G)][:].rearrange("p t m -> p m t"))

        def quantise_y(h, G):
            codes = rotating(("y_codes", h, G), [PART, PASS], U32, 3)
            nc.vector.quantize_mx(
                out=codes[:].bitcast(FP8X4), scales=y_scale[h][:, G, :],
                in_=held[("y_grouped", h, G)][:].rearrange("p m t -> p (m t)"),
            )
            nc.sync.dma_start(
                out=out_1[G].rearrange("p m t -> p (m t)")[:, h * 4 * PASS:(h + 1) * 4 * PASS].bitcast(I32),
                in_=codes[:].bitcast(I32),
            )
            if G == CG - 1:
                for q in range(4):
                    nc.sync.dma_start(
                        out=out_2[:, 4 * q:4 * q + 4, h * PASS:(h + 1) * PASS].rearrange("g r m -> r g m").bitcast(I32),
                        in_=y_scale[h][32 * q:32 * q + 4, :, :].bitcast(I32),
                    )

        def turn_y(h, G, j):
            bank = next_bank()
            held[("y_bank", h, G, j)] = bank
            for t in range(4):
                nc.tensor.transpose(bank[:, t * PART:(t + 1) * PART], held[("y_t", h, G)][:, t, j * PART:(j + 1) * PART], ident[:])

        def store_y(h, G, j, on_vector):
            rows = rotating(("y_rows", h, G, j), [PART, PART, 4], F32, 8)
            turned = held[("y_bank", h, G, j)][:].rearrange("r (t p) -> r p t", t=4)
            if on_vector:
                nc.vector.tensor_copy(out=rows[:], in_=turned)
            else:
                nc.scalar.copy(out=rows[:], in_=turned)
            r0 = (h * CHUNK_TILES + j) * PART
            nc.sync.dma_start(out=out_0[r0:r0 + PART, G * PASS:(G + 1) * PASS], in_=rows[:].rearrange("r p t -> r (p t)"))

        def later(f, *args):
            return lambda: f(*args)

        def requests(h, G, between=(), on_scalar=()):
            for t in range(4):
                request(h, G, t)
                if t < len(between):
                    for f in between[t]:
                        f()
                if t > 0:
                    limit(h, G, t - 1, t - 1 in on_scalar)

        def turn_and_store(h, G, on_vector):
            for j in range(CHUNK_TILES):
                turn_y(h, G, j)
                store_y(h, G, j, j in on_vector)

        def stage_one(i, fill_a, fill_b):
            signals(i, 0)
            if i + 1 < TILES:
                quantise_x(i + 1)
            subtract(i, 0)
            signals(i, 1)
            for f in fill_a:
                f()
            subtract(i, 1)
            weigh(i, 0)
            for f in fill_b:
                f()
            weigh(i, 1)

        def turns(i):
            if i >= 1:
                turn_e(i - 1)
            if i + 2 < TILES:
                turn_x(i + 2, 0)
                turn_x(i + 2, 1)
            if i + 3 in SORTED:
                sort_x(i + 3)

        turn_x(0, 0)
        turn_x(0, 1)
        quantise_x(0)
        turn_x(1, 0)
        turn_x(1, 1)
        quantise_x(1)
        for g in range(KG):
            signals(0, 0, [g])
            signals(0, 1, [g])
        spread_w()
        turns(0)
        subtract(0, 0)
        subtract(0, 1)
        order_a_scales(0)
        weigh(0, 0)
        weigh(0, 1)
        signals(1, 0)
        quantise_x(2)
        subtract(1, 0)
        signals(1, 1)
        order_a_words(0, 0)
        subtract(1, 1)
        weigh(1, 0)
        order_a_words(0, 1)
        weigh(1, 1)
        turns(1)
        fills = {
            2: ([later(quantise_e, 0), later(order_a_scales, 1)], [later(coil_constants, 0)]),
            3: ([later(quantise_e, 1), later(order_a_words, 1, 0), later(coil_constants, 1)], [later(coil_constants, 2)]),
            4: ([later(quantise_e, 2)], []),
        }
        for i in range(2, 5):
            stage_one(i, fills[i][0], fills[i][1])
            turns(i)
        quantise_e(3)
        stage_one(5, [], [later(order_a_scales, 2)])
        requests(0, 0, [[later(order_a_words, 1, 1)]], on_scalar=(0, 1))
        turns(5)
        limit(0, 0, 3)
        order_a_words(2, 0)
        quantise_e(4)
        stage_one(6, [later(group_y, 0, 0)], [])
        requests(0, 1, [[later(quantise_y, 0, 0), later(order_a_words, 2, 1)]], on_scalar=(0, 1))
        turn_e(5)
        limit(0, 1, 3)
        turn_and_store(0, 0, ())
        quantise_e(5)
        group_y(0, 1)
        stage_one(7, [later(quantise_y, 0, 1)], [])
        requests(0, 2, on_scalar=())
        turn_e(6, True)
        turn_e(7)
        limit(0, 2, 3)
        quantise_e(6)
        quantise_e(7)
        turn_and_store(0, 1, ())
        requests(1, 0, [[later(group_y, 0, 2)], [], [later(quantise_y, 0, 2)]])
        limit(1, 0, 3)
        turn_and_store(0, 2, (3,))
        requests(1, 1, [[later(group_y, 1, 0)], [], [later(quantise_y, 1, 0)]])
        limit(1, 1, 3)
        turn_and_store(1, 0, (3,))
        requests(1, 2, [[later(group_y, 1, 1)], [], [later(quantise_y, 1, 1)]])
        limit(1, 2, 3)
        turn_and_store(1, 1, ())
        group_y(1, 2)
        for j in range(4):
            turn_y(1, 2, j)
        store_y(1, 2, 0, False)
        quantise_y(1, 2)
        store_y(1, 2, 1, False)
        store_y(1, 2, 2, True)
        store_y(1, 2, 3, False)
